import numpy as np, ml_dtypes
CORES = [36,164,52,180,100,228,116,244]
N = 8
BF = ml_dtypes.bfloat16
def gentries(a):
    return np.ascontiguousarray(a.reshape(8, 16, -1).transpose(0, 2, 1)).reshape(8, -1)
def gtable(e):
    e = np.asarray(e); return np.ascontiguousarray(e.reshape(8, -1, 16).transpose(0, 2, 1)).reshape(128, -1).astype(np.int32)
def f(rng, *shape):
    return (rng.standard_normal(shape, dtype=np.float32) * np.exp2(rng.integers(-2, 3, shape[:-1] + (1,)))).astype(BF)
def wide(rng, *shape):
    v = f(rng, *shape).astype(np.float32); k = shape[:-2] + (1, shape[-1])
    return (v * np.exp2(rng.integers(-6, 7, k)) * (rng.random(k) > 0.0625)).astype(BF)
W, K, S, RO, FI, CAP = 3072, 768, 2, 3, 4, 96
def parts(rng):
    b = rng.random((N, 8, S, W)) < rng.choice(np.array([0.5, 0.6, 0.75]), (N, 8, S, 1)); b[..., 0] = True; b[..., W - 1] = True
    nx = np.zeros((N, 8, S, W), np.int64); cur = np.zeros((N, 8, S, K), np.int64)
    for a in range(N):
        for g in range(8):
            for i in range(S):
                v = np.nonzero(b[a, g, i])[0]
                nx[a, g, i] = rng.choice(v, W); nx[a, g, i, v] = rng.permutation(v); cur[a, g, i] = rng.choice(v, K)
    return b, nx, cur, rng.integers(0, S, (N, 8, K)), rng.integers(0, W, (N, 8, W))
def pack(x, b, nx, cur, typ, fro, w):
    mem = np.add.reduce(b.astype(np.int64) << np.arange(S)[:, None], axis=2)
    return {"x": x.astype(BF).reshape(N, 128, W), "nxt": nx.reshape(N, 8, S * W).astype(np.int32), "mem": mem.astype(np.int32), "fro": fro.astype(np.int32),
            "cur": np.stack([gtable(a.reshape(8, S * K)) for a in cur]), "typ": np.stack([gtable(a) for a in typ]), "w0": w.astype(BF).reshape(N, 128, K)}
def setup_inputs(rng):
    b, nx, cur, typ, fro = parts(rng)
    return pack(f(rng, N, 128, W), b, nx, cur, typ, fro, f(rng, N, 128, K))
def setup_inputs_room(rng):
    b, nx, cur, typ, fro = parts(rng)
    x = np.minimum(f(rng, N, 128, W).astype(np.float32), 24); w = f(rng, N, 128, K).astype(np.float32).reshape(N, 8, 16, K)
    w[:, ::2] = np.abs(w[:, ::2]) + 32; w[:, 1] = np.abs(w[:, 1]) + 32
    at = np.take_along_axis(cur, typ[:, :, None, :], 2)[:, :, 0]
    for q in range(FI): at = np.take_along_axis(nx.reshape(N, 8, S * W), typ * W + at, 2)
    z = np.where(typ == S - 1, 0, typ + 1)
    for a in range(N):
        m, zz, cc, i = at[a, 1], z[a, 1], cur[a, 1], a % S
        o = rng.permutation(np.arange(1, K - 1)); o = o[b[a, 1, zz[o], m[o]] & (m[o] > 0) & (m[o] < W - 2)]
        o = rng.permutation(o[np.unique(m[o], return_index=True)[1]])
        by = [o[zz[o] == j] for j in range(S)]
        cc[zz, np.arange(K)] = m
        for j in range(S): cc[j, by[j][:3]] = (0, W - 2, W - 1)
        u, v, p, q, e1, e2 = by[i][3:9]
        ends = [K - 1, 0] if a % 2 == 0 else [0, K - 1]
        typ[a, 1, ends] = typ[a, 1, [u, v]]; cc[:, ends] = cc[:, [u, v]]
        cc[i, ends[0]] = m[q]; cc[i, p] = m[v]
        r = rng.choice(np.nonzero(~b[a, 1, i, :W - 2])[0]); nx[a, 1, i, r] = nx[a, 1, i, m[e1]]; cc[i, e1] = r; cc[i, e2] = r
        b[a, 1, typ[a, 1, [u, p]], m[[u, p]]] = False
    for a in range(N):
        for g in range(0, 8, 2):
            m = at[a, g]; zz = z[a, g]; e = rng.permutation(np.nonzero(b[a, g, zz, m])[0])
            k = int(rng.choice(np.array([0, 1, CAP - 1, CAP, CAP + 1, len(e)])))
            if a < 2: k = ((CAP, CAP + 1, CAP - 1, 0), (1, CAP, len(e), CAP + 1))[a][g // 2]
            cur[a, g, zz[e], e] = m[e]
            one = e[(zz[e] == 0) & (m[e] != 0)][:1] if k == 1 else e[:0]
            e = np.concatenate([one, e])[:k]; k = len(e)
            c = rng.choice(np.concatenate([rng.permutation(W)[:int(rng.choice(np.array([24, 150, 600, W])))], m[e[:k // 4]]]), k)
            cur[a, g, zz[e], e] = np.where(c == m[e], (c + 1) % W, c)
            cur[a, g, 0, one] = 0
    return pack(x, b, nx, cur, typ, fro, w)
def setup_inputs_ties(rng):
    b, nx, cur, typ, fro = parts(rng)
    x = 4.0 * rng.integers(-3, 4, (N, 8, 16, W)); w = 4.0 * rng.integers(-3, 4, (N, 8, 16, K))
    x[::2, 5] = rng.choice(np.array([7.96875, 8, 8, 8, 8.0625]), (N // 2, 16, W)); x[1::2, 5] = 64
    w[:, 5] = rng.choice(np.array([-1.0, 1.0]), (N, 16, K)) * np.exp2(-1.0 * rng.integers(14, 21, (N, 16, K)))
    return pack(x, b, nx, cur, typ, fro, w)
def setup_inputs_alike(rng):
    b, nx, cur, typ, fro = parts(rng)
    cur[:, 0] = rng.choice(np.array([0, W - 1]), (N, S, K)); nx[:, 1] = rng.choice(np.array([0, 3, W // 2, W - 1]), (N, S, W)); nx[:, 2] = np.arange(W)
    fro[:, 3] = rng.choice(np.array([0, W - 1]), (N, W)); b[:, 4] = True; b[:, 5] = False; typ[:, 6] = 0; cur[:, 7] = np.repeat(cur[:, 7, :1], S, axis=1)
    return pack(f(rng, N, 128, W), b, nx, cur, typ, fro, f(rng, N, 128, K))
def setup_inputs_hot(rng):
    b, nx, cur, typ, fro = parts(rng)
    sh = rng.choice(np.array([-64, 0, 64]), (N, 8, 1, 1)); sh[0, :4, 0, 0] = (-64, 64, -64, 0); sh[1, 4:, 0, 0] = (0, -64, 64, -64)
    b[rng.random((N, 8)) < 0.3] = True; b[0, 0] = True; b[1, 5] = True
    x = f(rng, N, 128, W).reshape(N, 8, 16, W); w = f(rng, N, 128, K).astype(np.float32).reshape(N, 8, 16, K) + sh
    for g in (3, 6):
        b[:, g] = True; w[:, g] = 4
        x[::2, g] = (rng.integers(0, 25, x[::2, g].shape) * 0.125).astype(BF); x[1::2, g] = (rng.integers(-32, -7, x[1::2, g].shape) * 0.125).astype(BF)
    for a in range(0, N, 2):
        o = np.concatenate([CAP // 2 + rng.permutation(CAP // 2)[:CAP // 4], CAP + rng.permutation(K - CAP)[:CAP // 8]])
        w[a, 6][:, o] = 1000
    return pack(x, b, nx, cur, typ, fro, w)
def setup_inputs_spread(rng):
    b, nx, cur, typ, fro = parts(rng)
    return pack(wide(rng, N, 128, W), b, nx, cur, typ, fro, wide(rng, N, 128, K))
def check_inputs(d):
    bad = []
    for k, hi in (("nxt", W - 1), ("mem", 2 ** S - 1), ("fro", W - 1), ("cur", W - 1), ("typ", S - 1)):
        if np.min(d[k]) < 0 or np.max(d[k]) > hi: bad.append("range of " + k)
    for k in ("x", "w0"):
        if not np.all(np.abs(d[k].astype(np.float32)) < 2.0 ** 60): bad.append("size of " + k)
    return bad
def reference(x, nxt, mem, fro, cur, typ, w0):
    pick = np.take_along_axis
    X = x.astype(np.float32).reshape(N, 8, 16, W); w = w0.astype(np.float32).reshape(N, 8, 16, K)
    nx = nxt.astype(np.int64); mb = mem.astype(np.int64); fo = fro.astype(np.int64)
    c = np.stack([gentries(a) for a in cur]).astype(np.int64).reshape(N, 8, S, K); s = np.stack([gentries(a) for a in typ]).astype(np.int64)
    for t in range(RO):
        for q in range(FI):
            at = pick(c, s[:, :, None, :], 2)[:, :, 0]
            m = pick(nx, s * W + at, 2)
            hit = np.add.reduce((pick(X, m[:, :, None, :], 3) >= w).astype(np.int64), axis=2) >= 9
            bits = pick(mb, m, 2)
            for i in range(S): c[:, :, i] = np.where((s == i) | (hit & (((bits >> i) & 1) == 1)), m, c[:, :, i])
            s = np.where(hit, np.where(s == S - 1, 0, s + 1), s)
        z = np.where(s == S - 1, 0, s + 1)
        m = pick(c, s[:, :, None, :], 2)[:, :, 0]; e = pick(c, z[:, :, None, :], 2)[:, :, 0]
        want = (((pick(mb, m, 2) >> z) & 1) == 1) & (m != e)
        slot = want & (np.add.accumulate(want.astype(np.int64), axis=2) <= CAP)
        for a in range(N):
            for g in range(8):
                j = np.nonzero(slot[a, g])[0]
                p1 = z[a, g, j] * W + m[a, g, j]; p2 = z[a, g, j] * W + e[a, g, j]
                named = np.bincount(np.concatenate([p1, p2]), minlength=S * W)
                ok = (named[p1] == 1) & (named[p2] == 1); p1 = p1[ok]; p2 = p2[ok]
                v1 = nx[a, g, p1]; v2 = nx[a, g, p2]
                nx[a, g, p1] = v2; nx[a, g, p2] = v1
        k = pick(fo, m, 2)
        y = np.stack([pick(X[(a + 1 + t) % N], k[a][:, None, :], 2) for a in range(N)])
        w = w + np.minimum(np.maximum(y - w, np.float32(-8)), np.float32(8))
    return {"yc": np.stack([gtable(a.reshape(8, S * K)) for a in c]).astype(np.float32), "yw": w.reshape(N, 128, K).astype(np.float32), "yn": nx.astype(np.float32)}

@@ -1,0 +1,433 @@
+from concourse.mybir import AluOpType as A, ActivationFunctionType as F, AxisListType
+
+W, K, PL, DUM = 3072, 768, 6144, 6336
+F4, B2, I4, U2 = "float32", "bfloat16", "int32", "uint16"
+SCRATCH = {}
+for names, shape, dtype in (
+        ("XS XF0 XF1 XF2", [W], B2), ("XN NX", [DUM], B2), ("INFO Z", [PL], B2), ("N32", [DUM], F4), ("WW DD", [K], F4),
+        ("nb_", [24, 16], I4), ("nbf", [24, 16], F4), ("ld2 lt2", [24, 2, 16], F4), ("fr", [384], F4), ("LX", [384], U2),
+        ("memc froc", [192], I4), ("curc", [96], I4), ("typc", [48], I4), ("cl yco", [96], F4), ("cd", [48], F4), ("ti", [4, 192], I4),
+        ("T0 T1 TL M0 M1 M01 MT1 MT0 ML1 ML0 NM0 NM1 FH FL", [192], B2), ("ZR", [384], B2),
+        ("pc", [8], I4), ("pf", [8], F4), ("kr kg BL", [128], F4), ("tb", [192], F4), ("mk nbj nb1", [64], F4), ("dm0 dumL", [12], F4),
+        ("pi co", [16], F4), ("hm", [2], F4), ("CN", [24], B2), ("CK", [8], B2), ("CP G8", [16], B2), ("CB1 CB2", [128], B2), ("Mk", [4], F4),
+        ("DL", [24], F4), ("S96 I96 O96 DUMC", [96], B2), ("I6", [6], F4),
+        ("PO", [2, 2, 8, 4], F4), ("PI", [2, 2, 8, 4], I4), ("LP LO LD LK", [48], U2), ("ge nr RA RB", [K], B2),
+        ("t1", [2, 8, 4], F4), ("dd hd", [2, 16, 4], F4), ("TP TO TK", [2, 8, 4, 4], F4),
+        ("fl df d2 ne de", [2, 8, 4], F4), ("wt cs", [64], B2), ("rk wd", [64], F4), ("CC", [1536], B2),
+        ("RU", [192], U2), ("L6", [256], F4), ("Lf cnt tot nk tk Lq", [12], F4), ("eq", [12, 192], B2), ("jk gx gn", [192], B2), ("g32", [192], F4),
+        ("LE", [18], U2)):
+    for nm in names.split():
+        SCRATCH[nm] = ("sbuf", [128] + shape, dtype)
+PSUMS = ("N0", "N1", "C0", "C1", "XB", "L0", "L1", "XA")
+for nm in PSUMS:
+    SCRATCH[nm] = ("psum", [128, 512] if nm in ("L0", "L1", "XA") else [128, 128, 4], F4)
+SEMAPHORES = ["qv", "qp", "qs", "qg", "xl", "xa0", "xa1", "xa2"] + ["e%d" % k for k in range(12)] + ["d%d" % k for k in range(60)]
+AZ = "abcdefghijklmnopqrstuvwxyz"
+
+
+def rank_program(g, core, T, topo):
+    rank = T.rank_of(core)
+    if rank is None:
+        return
+    eng = {"v": g.vector, "p": g.tensor, "s": g.scalar, "g": g, "y": g.sync}
+    total, snap, last, reads, nd = {}, {}, {}, {}, {"d": 0, "e": 0}
+    know = {q: {} for q in eng}
+
+    def a(name, *idx, k=""):
+        t = T[name]
+        return (t[idx] if idx else t[:], [name + c for c in k] if k else [name])
+
+    def ind(win, off):
+        return (win[0].indirect(off[0]), win[1] + off[1])
+
+    def need(q, sem, val):
+        kn = know[q]
+        if kn.get(sem, 0) >= val:
+            return
+        eng[q].wait_ge(T.sem[sem], val)
+        for s2, v2 in snap.get((sem, val), {}).items():
+            kn[s2] = max(kn.get(s2, 0), v2)
+        kn[sem] = max(kn.get(sem, 0), val)
+
+    def deps(q, rd, wr, acc=False):
+        for key in rd + wr:
+            w = last.get(key)
+            if w is not None and not (acc and w[2] == q and key in wr):
+                need(q, w[0], w[1])
+            if key in PSUMS or key in wr:
+                for s2, (v2, q2) in list(reads.get(key, {}).items()):
+                    if q2 != q or s2[0] in "de":
+                        need(q, s2, v2)
+
+    def done(q, sem, val, rd, wr):
+        m = dict(know[q])
+        m[sem] = val
+        snap[(sem, val)] = m
+        for key in wr:
+            last[key] = (sem, val, q)
+            reads[key] = {}
+        for key in rd:
+            if key not in wr:
+                reads.setdefault(key, {})[sem] = (val, q)
+
+    def run(q, fn, outs, ins, acc=False):
+        rd = [x for i in ins for x in i[1]]
+        wr = [x for o in outs for x in o[1]]
+        deps(q, rd, wr, acc)
+        sem = "q" + q
+        total[sem] = total.get(sem, 0) + 1
+        fn().then_inc(T.sem[sem], 1)
+        done(q, sem, total[sem], rd, wr)
+
+    def dma(q, out, in_, **kw):
+        deps(q, in_[1], out[1])
+        c = "e" if q == "g" else "d"
+        sem = "%s%d" % (c, nd[c])
+        nd[c] += 1
+        total[sem] = 16
+        eng[q].dma_start(out[0], in_[0], **kw).then_inc(T.sem[sem], 16)
+        done(q, sem, 16, in_[1], out[1])
+
+    def tt(out, i0, i1, op):
+        run("v", lambda: g.vector.tensor_tensor(out[0], i0[0], i1[0], op), [out], [i0, i1])
+
+    def ts(out, i0, s1, op0, s2=None, op1=None):
+        ins = [i0] + [s for s in (s1, s2) if isinstance(s, tuple)]
+        x1 = s1[0] if isinstance(s1, tuple) else s1
+        x2 = s2[0] if isinstance(s2, tuple) else s2
+        more = [x2, op0] if op1 is None else [x2, op0, op1]
+        run("v", lambda: g.vector.tensor_scalar(out[0], i0[0], x1, *more), [out], ins)
+
+    def cp(out, i0):
+        run("v", lambda: g.vector.tensor_copy(out[0], i0[0]), [out], [i0])
+
+    def fill(out, v):
+        run("v", lambda: g.vector.memset(out[0], v), [out], [])
+
+    def act(out, i0, scale=None, bias=None, acc=None):
+        kw, ins, outs = {}, [i0], [out]
+        for nm, x in (("scale", scale), ("bias", bias)):
+            if isinstance(x, tuple):
+                ins.append(x)
+                kw[nm] = x[0]
+            elif x is not None:
+                kw[nm] = x
+        if acc is not None:
+            outs.append(acc)
+            kw["accum_out"] = acc[0]
+        fn = F.Identity if isinstance(bias, tuple) else F.Copy
+        run("s", lambda: g.scalar.activation(out[0], i0[0], fn, **kw), outs, ins)
+
+    def mm(out, lhsT, rhs, start=True, stop=True):
+        run("p", lambda: g.tensor.matmul(out[0], lhsT[0], rhs[0], start, stop), [out], [lhsT, rhs], acc=True)
+
+    def iota(out, pattern, base, cm, **kw):
+        run("g", lambda: g.iota(out[0], pattern, base, cm, **kw), [out], [])
+
+    ext = lambda ap: (ap, [])
+    al, R = slice(None), slice(0, 96)
+    cols = lambda nm, lo, hi, k="": a(nm, al, slice(lo, hi), k=k)
+    col = lambda nm, j: a(nm, al, slice(j, j + 1))
+    half = lambda nm, b: cols(nm, 384 * b, 384 * b + 384, k=str(b))
+
+    dma("s", a("nb_"), ext(T.nxt[:]))
+    dma("y", a("memc"), ext(T.mem[:]))
+    dma("s", a("curc"), ext(T.cur[:]))
+    dma("y", a("froc"), ext(T.fro[:]))
+    dma("s", a("typc"), ext(T.typ[:]))
+    dma("y", a("XS"), ext(T.x[:]))
+
+    fl_ = {"allow_small_or_imprecise_dtypes": True}
+    iota(col("pc", 0), [[0, 1]], 0, 1)
+    iota(a("tb"), [[64, 3], [0, 64]], 0, 0, **fl_)
+    iota(a("TL"), [[0, 3], [1, 64]], 0, 0, **fl_)
+    iota(a("kr"), [[1, 128]], 0, 0, **fl_)
+    dma("g", a("WW", k="01"), ext(T.w0[:]))
+    iota(a("kg"), [[1, 8], [0, 16]], 0, 0, **fl_)
+    iota(a("mk"), [[0, 16], [1, 4]], 0, 0, **fl_)
+    iota(a("nbj"), [[384, 2], [0, 8], [1, 4]], 768, 4, **fl_)
+    iota(a("nb1"), [[384, 2], [0, 8], [1, 4]], 769, 4, **fl_)
+    iota(a("dm0"), [[96, 2], [16, 6]], 6144, 0, **fl_)
+    for j, op in ((1, (15, A.bitwise_and)),
+                  (2, (4, A.arith_shift_right)),
+                  (3, (3, A.bitwise_and)), (4, (2, A.arith_shift_right)),
+                  (5, (4, A.arith_shift_right, 1, A.bitwise_and))):
+        ts(col("pc", j), col("pc", 0), *op)
+    cp(cols("pf", 0, 6), cols("pc", 0, 6))
+    p0, pm, gi = col("pf", 0), col("pf", 1), col("pf", 2)
+    ts(col("pf", 6), pm, 192.0, A.mult)
+    ts(col("hm", 0), col("pf", 5), -1.0, A.mult, 1.0, A.add)
+    ts(a("T0"), a("tb"), col("pf", 6), A.add)
+    ts(a("T1"), a("T0"), 3072.0, A.add)
+    act(cols("L0", 0, 192), a("T0"))
+    act(cols("L0", 192, 384), a("T1"))
+    act(cols("L1", 0, 192), a("TL"))
+    fill(a("ZR"), 0.0)
+    ts(a("pi"), cols("kr", 0, 16), pm, A.is_equal)
+    ts(cols("G8", 0, 8), cols("kr", 0, 8), gi, A.is_equal)
+    co, pi = (lambda j: col("co", j)), (lambda j: col("pi", j))
+    g8 = cols("G8", 0, 8)
+    act(co(7), pi(4), scale=0.25)
+    act(co(1), pi(0), bias=pi(1))
+    act(co(0), co(1), bias=co(7))
+    act(co(10), pi(2), bias=pi(3))
+    act(co(11), co(10), bias=pi(5))
+    act(co(12), co(0), scale=-1.0)
+    act(co(2), co(11), bias=co(12))
+    act(cols("CN", 0, 8), g8, scale=co(0))
+    act(cols("CN", 8, 16), g8, scale=pi(6))
+    act(cols("CN", 16, 24), g8, scale=co(2))
+    act(cols("G8", 8, 16), g8)
+    ts(a("Mk"), cols("kr", 0, 4), col("pf", 3), A.is_equal)
+    ts(a("DL"), cols("kr", 0, 24), col("pf", 4), A.is_equal)
+
+    ti = lambda j: a("ti", al, j, al, k=str(j))
+    ts(ti(0), a("memc"), 1, A.bitwise_and)
+    ts(ti(1), a("memc"), 1, A.arith_shift_right)
+    cp(a("M0"), ti(0))
+    cp(a("M1"), ti(1))
+    cp(a("nbf"), a("nb_"))
+    tt(a("MT1"), a("M1"), cols("L0", 192, 384), A.mult)
+    tt(a("MT0"), a("M0"), cols("L0", 0, 192), A.mult)
+    tt(a("ML1"), a("M1"), cols("L1", 0, 192), A.mult)
+    tt(a("ML0"), a("M0"), cols("L1", 0, 192), A.mult)
+    act(a("ld2", al, al, 0, al, k="0"), a("nbf"), scale=col("hm", 0))
+    act(a("ld2", al, al, 1, al, k="1"), a("nbf"), scale=col("pf", 5))
+    act(a("NM0"), a("M0"), scale=-1.0, bias=1.0)
+    act(a("NM1"), a("M1"), scale=-1.0, bias=1.0)
+    act(cols("L1", 192, 384), a("M1"), scale=0.25)
+    ts(ti(2), a("froc"), 6, A.arith_shift_right)
+    ts(ti(3), a("froc"), 63, A.bitwise_and)
+    ts(a("FH"), ti(2), 64.0, A.mult)
+    cp(a("FL"), ti(3))
+    tt(a("M01"), a("M0"), cols("L1", 192, 384), A.mult)
+    for n in range(6):
+        dma("y", (T.INFO[10 + n:128:16, :], ["INFO" + AZ[20 + n]]), a("ZR"))
+    for r, lo, hi in ((0, "T0", "T1"), (1, "TL", "TL"), (7, "T1", "T0"), (4, "M1", "M0"), (2, "MT1", "MT0"), (3, "ML1", "ML0"), (6, "NM1", "NM0"),
+                      (8, "FH", "FH"), (9, "FL", "FL"), (5, "M01", "M01")):
+        for h, nm in enumerate((lo, hi)):
+            dma("sy"[h], (T.INFO[r:128:16, W * h:W * h + W], ["INFO" + AZ[2 * r + h]]), a(nm))
+    info = lambda lo, hi: cols("INFO", lo, hi, k=AZ)
+
+    run("v", lambda: g.vector.transpose(T.lt2[:], T.ld2[:]), [a("lt2")], [a("ld2", k="01")])
+    lx = lambda h: cols("LX", 192 * h, 192 * h + 192, k=str(h))
+    for h in range(2):
+        for ch in range(8 * h, 8 * h + 8):
+            tt(cols("fr", 24 * ch, 24 * ch + 24, k=AZ[ch]), a("lt2", al, al, 0, ch), a("lt2", al, al, 1, ch), A.add)
+        cp(lx(h), cols("fr", 192 * h, 192 * h + 192, k=AZ[8 * h:8 * h + 8]))
+    fill(cols("NX", PL, DUM), 0.0)
+    fill(cols("XN", PL, DUM), 0.0)
+    for h in range(2):
+        cp(cols("XN", W * h, W * h + W), ind(a("XS"), lx(h)))
+        act(cols("NX", W * h, W * h + W), ind(info(W * h, W * h + W), lx(h)))
+
+    lo_, hi_ = cols("cl", 0, 48), cols("cl", 48, 96)
+    cp(a("cl"), a("curc"))
+    ts(hi_, hi_, 3072.0, A.add)
+    tt(a("cd"), hi_, lo_, A.subtract)
+    tt(a("cd"), a("cd"), a("typc"), A.mult)
+    tt(lo_, lo_, a("cd"), A.add)
+    tt(hi_, hi_, a("cd"), A.subtract)
+    cp(a("LP", k="01"), lo_)
+    cp(a("LO", k="01"), hi_)
+    l24 = lambda nm, b: cols(nm, 24 * b, 24 * b + 24, k=str(b))
+    cp(half("RB", 0), ind(info(0, PL), l24("LO", 0)))
+    act(half("RB", 1), ind(info(0, PL), l24("LO", 1)))
+
+    deps("g", ["XS"], [])
+    for t in range(3):
+        dst = T.cores[(rank - 1 - t) % 8]
+        rid, pid = topo.addr(dst, core)
+        n = len(topo.engines(core, dst))
+        sem = "xa%d" % t
+        total["xl"] = total.get("xl", 0) + n
+        total[sem] = n
+        g.remote_dma(T["XF%d" % t][:], T.XS[:], T.sem[sem], T.sem.xl, pid, rid, topo.mask(core, dst))
+        last["XF%d" % t] = (sem, n, "-")
+    iota(a("Z"), [[0, PL]], 0, 0, **fl_)
+    iota(a("N32"), [[0, DUM]], 0, 0, **fl_)
+    for k, (r, h, nm) in enumerate(((10, 0, "T0"), (10, 1, "T1"), (11, 0, "TL"), (11, 1, "TL"))):
+        deps("y", [], ["Z"])
+        dma("y", (T.Z[r:128:16, W * h:W * h + W], ["Z" + AZ[k]]), a(nm))
+
+    def tform(bank, c0, n, rowbuf, b, rhs):
+        for i1 in range(4):
+            mm(a(bank, R, slice(c0, c0 + n), i1), a(rowbuf, al, slice(384 * b + i1, 384 * b + 384, 4), k=str(b)), rhs)
+
+    def pads(tp, b, src, nv):
+        for i0 in range(4):
+            out, m = a(tp, R, b, al, i0, al, k=str(4 * b + i0)), a("Mk", R, slice(i0, i0 + 1))
+            if i0 < nv:
+                ts(out, src, m, A.mult)
+            else:
+                act(out, src, scale=m)
+
+    def tolist(bank, c0, tp, b):
+        mm(cols(bank, c0, c0 + 24), (T[tp][0:96, b], [tp + str(4 * b + i) for i in range(4)]), a("DL", R))
+
+    ot = lambda b: (T.PO[0:96, b, 0], ["PO%d" % b])
+    pt = lambda b: (T.PO[0:96, b, 1], ["PO%d" % b])
+    for b in range(2):
+        tform("XB", 8 * b, 8, "RB", b, cols("CN", 0, 8))
+        cp(ot(b), a("XB", R, slice(8 * b, 8 * b + 8), al))
+
+    def start(b):
+        off, gew, ww = l24("LP", b), half("ge", b), half("WW", b)
+        tt(gew, ind(a("XN"), off), ww, A.is_ge)
+        act(a("N%d" % b, R, slice(0, 8), al), ot(b))
+        act(half("nr", b), ind(a("NX"), off))
+        tform("N%d" % b, 8, 24, "nr", b, a("CN"))
+
+    def part0(b):
+        N, k = "N%d" % b, str(b)
+        t1, dO, dP = a("t1", R, b, k=k), (T.dd[0:96, b, 0:8, :], ["dd" + k]), (T.dd[0:96, b, 8:16, :], ["dd" + k])
+        tt(t1, a(N, R, slice(16, 24), al), ot(b), A.mult)
+        tt(dO, a(N, R, slice(8, 16), al), ot(b), A.subtract)
+        tt(dP, a(N, R, slice(24, 32), al), t1, A.add)
+
+    def part1(b, nv=2):
+        C, N, k = "C%d" % b, "N%d" % b, str(b)
+        ts(a(C, R, slice(32, 48), al), a(C, R, slice(0, 16), al), 8.5, A.is_ge)
+        tt(a("hd", R, b, k=k), a(C, R, slice(32, 48), al), a("dd", R, b, k=k), A.mult)
+        tt((T.PO[0:96, b], ["PO" + k]), a(N, R, slice(0, 16), al), a("hd", R, b, k=k), A.add)
+        pads("TP", b, pt(b), nv)
+        tolist("L%d" % b, 0, "TP", b)
+
+    def part2(b):
+        cp(l24("LP", b), cols("L%d" % b, 0, 24))
+
+    def late_constants():
+        for j, i, k in ((3, 8, 9), (4, 7, 1), (5, 10, 11), (6, 1, 11)):
+            act(co(j), pi(i), bias=pi(k))
+        act(co(8), pi(7), scale=6144.0)
+        act(co(9), pi(10), scale=6240.0)
+        act(co(13), co(8), bias=co(9))
+        act(a("CK"), g8, scale=co(3))
+        act(cols("CP", 0, 8), g8, scale=co(4))
+        act(cols("CP", 8, 16), g8, scale=co(5))
+        ts(a("BL"), a("kg"), gi, A.is_equal)
+        act(a("CB1"), a("BL"), scale=co(4))
+        act(a("CB2"), a("BL"), scale=co(5))
+        ts(a("mk"), a("mk"), 0.5, A.is_ge)
+        ts(a("I96"), cols("kr", 0, 96), p0, A.is_equal)
+        ts(a("S96"), cols("kr", 0, 96), p0, A.is_gt)
+        fill(a("O96"), 1.0)
+        ts(a("I6"), cols("kr", 0, 6), p0, A.is_equal)
+        ts(a("DUMC"), cols("kr", 0, 96), co(6), A.mult, co(13), A.add)
+        ts(a("dumL"), a("dm0"), pm, A.add)
+
+    for t in range(3):
+        prev = None
+        for q in range(4):
+            for b in range(2):
+                start(b)
+                if prev is not None:
+                    part1(prev)
+                tform("C%d" % b, 0, 16, "ge", b, a("G8"))
+                part0(b)
+                if prev is not None:
+                    part2(prev)
+                prev = b
+            if t == 0 and q == 0:
+                late_constants()
+        pads("TO", 0, ot(0), 0)
+        tolist("L0", 64, "TO", 0)
+        part1(1, 4)
+        act(half("RA", 0), ind(info(0, PL), l24("LP", 0)))
+        pads("TO", 1, ot(1), 0)
+        tolist("L0", 88, "TO", 1)
+        part2(1)
+        act(half("RA", 1), ind(info(0, PL), l24("LP", 1)))
+
+        x01 = ["PO0", "PO1"]
+        cp((T.PI[0:96], ["PI"]), (T.PO[0:96], x01))
+        tt(a("fl", R), (T.PO[0:96, :, 1], x01), (T.PI[0:96, :, 1], ["PI"]), A.subtract)
+        tt(a("df", R), (T.PI[0:96, :, 0], ["PI"]), (T.PI[0:96, :, 1], ["PI"]), A.subtract)
+        tt(a("d2", R), a("df", R), a("df", R), A.mult)
+        ts(a("ne", R), a("d2", R), 9437184.0, A.not_equal, 4.0, A.mult)
+        tt(a("wt", R), a("fl", R), a("ne", R), A.mult)
+        run("v", lambda: g.vector.tensor_tensor_scan(T.cs[0:96, :], T.mk[0:96, :], T.wt[0:96, :], 0.0, A.mult, A.add), [a("cs")], [a("mk"), a("wt")])
+        cp(a("LO", k="01"), cols("L0", 64, 112))
+        for b in range(2):
+            act(half("RB", b), ind((T.Z[:], ["Z", "Za", "Zb", "Zc", "Zd"]), l24("LO", b)))
+        mm(a("XA", R, slice(0, 64)), a("I96", R), a("cs", R), True, False)
+        for i1 in range(4):
+            mm(a("XA", R, slice(i1, 64, 4)), a("S96", R), a("cs", R, slice(3, 64, 4)), False, False)
+            mm(a("XA", R, slice(32 + i1, 64, 4)), a("O96", R), a("cs", R, slice(3, 32, 4)), False, i1 == 3)
+        tt(a("rk", R), a("XA", R, slice(0, 64)), a("nb1", R), A.subtract)
+        tt(a("wd", R), a("wt", R), a("rk", R), A.mult)
+        tt(a("de", R), a("wd", R), a("nbj", R), A.add)
+        for b in range(2):
+            pads("TP", b, (T.de[0:96, b], ["de"]), 4)
+            tolist("L1", 24 * b, "TP", b)
+        cp(cols("CC", 0, 96), a("DUMC"))
+        cp(a("LD"), cols("L1", 0, 48))
+        tt(ind(a("CC"), a("LD"))[:1] + (["CC"],), a("RA", k="01"), (T.RB[:], ["RB0", "RB1", "LD"]), A.add)
+        for b in range(2):
+            tform("XB", 8 * b, 8, "RA", b, a("CK"))
+        for b in range(2):
+            pads("TK", b, a("XB", R, slice(8 * b, 8 * b + 8), al), 0)
+            tolist("L0", 24 * b, "TK", b)
+        for i in range(16):
+            mm(a("L1", slice(0, 6), slice(i, 256, 16)), a("CC", al, slice(i, 96, 16)), a("CP"))
+        mm(cols("XA", 128, 224), a("CB1"), cols("CC", 0, 96))
+        mm(cols("XA", 224, 320), a("CB2"), cols("CC", 0, 96))
+        act(a("L6", slice(0, 6)), a("L1", slice(0, 6), slice(0, 256)))
+        for k in range(2):
+            mm(cols("L1", 256 + 6 * k, 262 + 6 * k), a("L6", slice(0, 6), slice(128 * k, 128 * k + 128)), a("I6", slice(0, 6)))
+        cp(a("LK"), cols("L0", 0, 48))
+
+        def pull(b):
+            tt(half("DD", b), ind(a("XF%d" % t), cols("LK", 24 * b, 24 * b + 24)), half("WW", b), A.subtract)
+
+        def addw(b):
+            ts(half("DD", b), half("DD", b), 8.0, A.min, -8.0, A.max)
+            dma("g", half("WW", b), half("DD", b), accum_op=A.add)
+        pull(0)
+        addw(0)
+        cp(a("RU"), cols("XA", 128, 320))
+        pull(1)
+        cp(a("Lf"), cols("L1", 256, 268))
+        SN = 9
+        for k in range(12):
+            ts(a("eq", al, k, k=AZ[k]), a("RU"), col("Lf", k), A.is_equal)
+            if k < SN:
+                act(a("jk"), a("eq", al, k, k=AZ[k]), acc=cols("cnt", k, k + 1, k=AZ[k]))
+        addw(1)
+        for k in range(SN, 12):
+            run("v", lambda k=k: g.vector.tensor_reduce(T.cnt[:, k:k + 1], T.eq[:, k, :], AxisListType.X, A.add), [a("cnt", k=AZ[k])], [a("eq", k=AZ[k])])
+        c0, c1 = cols("cnt", 0, 6, k=AZ[:6]), cols("cnt", 6, 12, k=AZ[6:12])
+        tt(cols("tot", 0, 6), c0, c1, A.add)
+        tt(cols("tot", 6, 12), c0, c1, A.add)
+        ts(a("nk"), a("tot"), 2.5, A.is_ge)
+        tt(a("tk"), a("nk"), a("dumL"), A.mult)
+        tt(a("Lq"), a("Lf"), a("tk"), A.max)
+        cp(cols("LE", 0, 12, k="0"), a("Lq"))
+        cp(cols("LE", 12, 18, k="1"), cols("Lq", 0, 6))
+        le0, le1 = cols("LE", 0, 12, k="0"), cols("LE", 6, 18, k="01")
+
+        def put(win, src):
+            run("v", lambda: g.vector.tensor_copy(T[win][:].indirect(le1[0]), src[0]), [a(win)], [src, le1])
+        if t < 2:
+            act(a("gn"), ind(a("NX"), le0))
+            cp(a("gx"), ind(a("XN"), le0))
+            put("NX", a("gn"))
+            put("XN", a("gx"))
+            if t == 1:
+                n8 = lambda nm, r, lo, hi: a(nm, slice(r, 128, 16), slice(lo, hi))
+                dma("g", n8("N32", 0, 0, W), n8("NX", 0, 0, W))
+                dma("g", n8("N32", 0, W, PL), n8("NX", 7, W, PL))
+                dma("g", n8("N32", 0, 0, PL), n8("NX", 1, 0, PL), accum_op=A.add, max_dma_last_dim=4096)
+        else:
+            cp(a("g32"), ind(a("N32"), le0))
+            put("N32", a("g32"))
+            dma("y", ext(T.yn[:]), a("N32", slice(0, 128, 16), slice(0, PL)))
+            dma("s", ext(T.yw[:]), a("WW", k="01"))
+            cp(lo_, a("LP", k="01"))
+            cp(hi_, a("LO", k="01"))
+            tt(cols("yco", 0, 48), lo_, hi_, A.min)
+            tt(cols("yco", 48, 96), lo_, hi_, A.max)
+            ts(cols("yco", 48, 96), cols("yco", 48, 96), -3072.0, A.add)
+            dma("s", ext(T.yc[:]), a("yco"))
+    for sem, val in total.items():
+        need("g", sem, val)

@@ -6,7 +6,7 @@ SCRATCH = {}
 for names, shape, dtype in (
         ("XS XF0 XF1 XF2", [W], B2), ("XN NX", [DUM], B2), ("INFO Z", [PL], B2), ("N32", [DUM], F4), ("WW DD", [K], F4),
         ("nb_", [24, 16], I4), ("nbf", [24, 16], F4), ("ld2 lt2", [24, 2, 16], F4), ("fr", [384], F4), ("LX", [384], U2),
-        ("memc froc", [192], I4), ("curc", [96], I4), ("typc", [48], I4), ("cl yco", [96], F4), ("cd", [48], F4), ("ti", [4, 192], I4),
+        ("memc froc", [192], I4), ("curc", [96], I4), ("typc", [48], I4), ("cl yco", [96], F4), ("cd cx cp cq", [48], F4), ("ti", [4, 192], I4),
         ("T0 T1 TL M0 M1 M01 MT1 MT0 ML1 ML0 NM0 NM1 FH FL", [192], B2), ("ZR", [384], B2),
         ("pc", [8], I4), ("pf", [8], F4), ("kr kg BL", [128], F4), ("tb", [192], F4), ("mk nbj nb1", [64], F4), ("dm0 dumL", [12], F4),
         ("pi co", [16], F4), ("hm", [2], F4), ("CN", [24], B2), ("CK", [8], B2), ("CP G8", [16], B2), ("CB1 CB2", [128], B2), ("Mk", [4], F4),
@@ -14,8 +14,8 @@ for names, shape, dtype in (
         ("PO", [2, 2, 8, 4], F4), ("PI", [2, 2, 8, 4], I4), ("LP LO LD LK", [48], U2), ("ge nr RA RB", [K], B2),
         ("t1", [2, 8, 4], F4), ("dd hd", [2, 16, 4], F4), ("TP TO TK", [2, 8, 4, 4], F4),
         ("fl df d2 ne de", [2, 8, 4], F4), ("wt cs", [64], B2), ("rk wd", [64], F4), ("CC", [1536], B2),
-        ("RU", [192], U2), ("L6", [256], F4), ("Lf cnt tot nk tk Lq", [12], F4), ("eq", [12, 192], B2), ("jk gx gn", [192], B2), ("g32", [192], F4),
-        ("LE", [18], U2)):
+        ("RU", [192], U2), ("L6", [256], F4), ("Lf tk Lq", [12], F4), ("tot nk", [6], F4), ("eq", [2304], B2), ("jk", [1536], B2),
+        ("gx gn", [192], B2), ("g32", [192], F4), ("LE", [18], U2)):
     for nm in names.split():
         SCRATCH[nm] = ("sbuf", [128] + shape, dtype)
 PSUMS = ("N0", "N1", "C0", "C1", "XB", "L0", "L1", "XA")
@@ -23,6 +23,7 @@ for nm in PSUMS:
     SCRATCH[nm] = ("psum", [128, 512] if nm in ("L0", "L1", "XA") else [128, 128, 4], F4)
 SEMAPHORES = ["qv", "qp", "qs", "qg", "xl", "xa0", "xa1", "xa2"] + ["e%d" % k for k in range(12)] + ["d%d" % k for k in range(60)]
 AZ = "abcdefghijklmnopqrstuvwxyz"
+SEQ, NV = "st C PO' pd' ls' t1 dO dP hh LP' hd".split(), 2
 
 
 def rank_program(g, core, T, topo):
@@ -127,8 +128,9 @@ def rank_program(g, core, T, topo):
     ext = lambda ap: (ap, [])
     al, R = slice(None), slice(0, 96)
     cols = lambda nm, lo, hi, k="": a(nm, al, slice(lo, hi), k=k)
-    col = lambda nm, j: a(nm, al, slice(j, j + 1))
+    col = lambda nm, j: a(nm, al, slice(j, j + 1), k=AZ[j])
     half = lambda nm, b: cols(nm, 384 * b, 384 * b + 384, k=str(b))
+    l24 = lambda nm, b: cols(nm, 24 * b, 24 * b + 24, k=str(b))
 
     dma("s", a("nb_"), ext(T.nxt[:]))
     dma("y", a("memc"), ext(T.mem[:]))
@@ -153,7 +155,7 @@ def rank_program(g, core, T, topo):
                   (3, (3, A.bitwise_and)), (4, (2, A.arith_shift_right)),
                   (5, (4, A.arith_shift_right, 1, A.bitwise_and))):
         ts(col("pc", j), col("pc", 0), *op)
-    cp(cols("pf", 0, 6), cols("pc", 0, 6))
+    cp(cols("pf", 0, 6, k=AZ[:6]), cols("pc", 0, 6, k=AZ[:6]))
     p0, pm, gi = col("pf", 0), col("pf", 1), col("pf", 2)
     ts(col("pf", 6), pm, 192.0, A.mult)
     ts(col("hm", 0), col("pf", 5), -1.0, A.mult, 1.0, A.add)
@@ -163,10 +165,10 @@ def rank_program(g, core, T, topo):
     act(cols("L0", 192, 384), a("T1"))
     act(cols("L1", 0, 192), a("TL"))
     fill(a("ZR"), 0.0)
-    ts(a("pi"), cols("kr", 0, 16), pm, A.is_equal)
-    ts(cols("G8", 0, 8), cols("kr", 0, 8), gi, A.is_equal)
+    ts(a("pi", k=AZ[:16]), cols("kr", 0, 16), pm, A.is_equal)
+    ts(cols("G8", 0, 8, k="0"), cols("kr", 0, 8), gi, A.is_equal)
     co, pi = (lambda j: col("co", j)), (lambda j: col("pi", j))
-    g8 = cols("G8", 0, 8)
+    g8 = cols("G8", 0, 8, k="0")
     act(co(7), pi(4), scale=0.25)
     act(co(1), pi(0), bias=pi(1))
     act(co(0), co(1), bias=co(7))
@@ -174,10 +176,10 @@ def rank_program(g, core, T, topo):
     act(co(11), co(10), bias=pi(5))
     act(co(12), co(0), scale=-1.0)
     act(co(2), co(11), bias=co(12))
-    act(cols("CN", 0, 8), g8, scale=co(0))
-    act(cols("CN", 8, 16), g8, scale=pi(6))
-    act(cols("CN", 16, 24), g8, scale=co(2))
-    act(cols("G8", 8, 16), g8)
+    act(cols("CN", 0, 8, k="0"), g8, scale=co(0))
+    act(cols("CN", 8, 16, k="1"), g8, scale=pi(6))
+    act(cols("CN", 16, 24, k="2"), g8, scale=co(2))
+    act(cols("G8", 8, 16, k="1"), g8)
     ts(a("Mk"), cols("kr", 0, 4), col("pf", 3), A.is_equal)
     ts(a("DL"), cols("kr", 0, 24), col("pf", 4), A.is_equal)
 
@@ -196,10 +198,19 @@ def rank_program(g, core, T, topo):
     act(a("NM0"), a("M0"), scale=-1.0, bias=1.0)
     act(a("NM1"), a("M1"), scale=-1.0, bias=1.0)
     act(cols("L1", 192, 384), a("M1"), scale=0.25)
+    lo_, hi_ = cols("cl", 0, 48, k="0"), cols("cl", 48, 96, k="1")
+    cp(lo_, cols("curc", 0, 48))
+    ts(hi_, cols("curc", 48, 96), 3072.0, A.add)
     ts(ti(2), a("froc"), 6, A.arith_shift_right)
+    tt(a("cd"), hi_, lo_, A.subtract)
     ts(ti(3), a("froc"), 63, A.bitwise_and)
+    tt(a("cx"), a("cd"), a("typc"), A.mult)
     ts(a("FH"), ti(2), 64.0, A.mult)
+    tt(a("cp"), lo_, a("cx"), A.add)
+    tt(a("cq"), hi_, a("cx"), A.subtract)
     cp(a("FL"), ti(3))
+    cp(a("LP", k="01"), a("cp"))
+    cp(a("LO", k="01"), a("cq"))
     tt(a("M01"), a("M0"), cols("L1", 192, 384), A.mult)
     for n in range(6):
         dma("y", (T.INFO[10 + n:128:16, :], ["INFO" + AZ[20 + n]]), a("ZR"))
@@ -215,27 +226,20 @@ def rank_program(g, core, T, topo):
         for ch in range(8 * h, 8 * h + 8):
             tt(cols("fr", 24 * ch, 24 * ch + 24, k=AZ[ch]), a("lt2", al, al, 0, ch), a("lt2", al, al, 1, ch), A.add)
         cp(lx(h), cols("fr", 192 * h, 192 * h + 192, k=AZ[8 * h:8 * h + 8]))
-    fill(cols("NX", PL, DUM), 0.0)
-    fill(cols("XN", PL, DUM), 0.0)
+    fill(cols("NX", PL, DUM, k="2"), 0.0)
+    fill(cols("XN", PL, DUM, k="2"), 0.0)
     for h in range(2):
-        cp(cols("XN", W * h, W * h + W), ind(a("XS"), lx(h)))
-        act(cols("NX", W * h, W * h + W), ind(info(W * h, W * h + W), lx(h)))
+        cp(cols("XN", W * h, W * h + W, k=str(h)), ind(a("XS"), lx(h)))
+        act(cols("NX", W * h, W * h + W, k=str(h)), ind(info(W * h, W * h + W), lx(h)))
+        if h == 0:
+            cp(half("RB", 0), ind(info(0, PL), l24("LO", 0)))
+            act(half("RB", 1), ind(info(0, PL), l24("LO", 1)))
+    XN, NX = a("XN", k="012"), a("NX", k="012")
 
-    lo_, hi_ = cols("cl", 0, 48), cols("cl", 48, 96)
-    cp(a("cl"), a("curc"))
-    ts(hi_, hi_, 3072.0, A.add)
-    tt(a("cd"), hi_, lo_, A.subtract)
-    tt(a("cd"), a("cd"), a("typc"), A.mult)
-    tt(lo_, lo_, a("cd"), A.add)
-    tt(hi_, hi_, a("cd"), A.subtract)
-    cp(a("LP", k="01"), lo_)
-    cp(a("LO", k="01"), hi_)
-    l24 = lambda nm, b: cols(nm, 24 * b, 24 * b + 24, k=str(b))
-    cp(half("RB", 0), ind(info(0, PL), l24("LO", 0)))
-    act(half("RB", 1), ind(info(0, PL), l24("LO", 1)))
-
-    deps("g", ["XS"], [])
-    for t in range(3):
+    def sendx(t):
+        deps("g", ["XS"], [])
+        if t:
+            need("g", "xl", total["xl"])
         dst = T.cores[(rank - 1 - t) % 8]
         rid, pid = topo.addr(dst, core)
         n = len(topo.engines(core, dst))
@@ -244,18 +248,22 @@ def rank_program(g, core, T, topo):
         total[sem] = n
         g.remote_dma(T["XF%d" % t][:], T.XS[:], T.sem[sem], T.sem.xl, pid, rid, topo.mask(core, dst))
         last["XF%d" % t] = (sem, n, "-")
+    sendx(0)
     iota(a("Z"), [[0, PL]], 0, 0, **fl_)
     iota(a("N32"), [[0, DUM]], 0, 0, **fl_)
     for k, (r, h, nm) in enumerate(((10, 0, "T0"), (10, 1, "T1"), (11, 0, "TL"), (11, 1, "TL"))):
         deps("y", [], ["Z"])
         dma("y", (T.Z[r:128:16, W * h:W * h + W], ["Z" + AZ[k]]), a(nm))
+    zz = (T.Z[:], ["Z", "Za", "Zb", "Zc", "Zd"])
 
     def tform(bank, c0, n, rowbuf, b, rhs):
         for i1 in range(4):
             mm(a(bank, R, slice(c0, c0 + n), i1), a(rowbuf, al, slice(384 * b + i1, 384 * b + 384, 4), k=str(b)), rhs)
 
-    def pads(tp, b, src, nv):
+    def pads(tp, b, src, nv, between=()):
         for i0 in range(4):
+            if i0 in (1, 3) and between:
+                between[i0 // 2]()
             out, m = a(tp, R, b, al, i0, al, k=str(4 * b + i0)), a("Mk", R, slice(i0, i0 + 1))
             if i0 < nv:
                 ts(out, src, m, A.mult)
@@ -268,33 +276,46 @@ def rank_program(g, core, T, topo):
     ot = lambda b: (T.PO[0:96, b, 0], ["PO%d" % b])
     pt = lambda b: (T.PO[0:96, b, 1], ["PO%d" % b])
     for b in range(2):
-        tform("XB", 8 * b, 8, "RB", b, cols("CN", 0, 8))
+        tform("XB", 8 * b, 8, "RB", b, cols("CN", 0, 8, k="0"))
         cp(ot(b), a("XB", R, slice(8 * b, 8 * b + 8), al))
 
     def start(b):
         off, gew, ww = l24("LP", b), half("ge", b), half("WW", b)
-        tt(gew, ind(a("XN"), off), ww, A.is_ge)
+        tt(gew, ind(XN, off), ww, A.is_ge)
         act(a("N%d" % b, R, slice(0, 8), al), ot(b))
-        act(half("nr", b), ind(a("NX"), off))
-        tform("N%d" % b, 8, 24, "nr", b, a("CN"))
+        c, k2 = 384 * b, (str(b), "xy"[b])
+        act(cols("nr", c, c + 256, k=k2[0]), ind(NX, cols("LP", 24 * b, 24 * b + 16, k=str(b))))
+        act(cols("nr", c + 256, c + 384, k=k2[1]), ind(NX, cols("LP", 24 * b + 16, 24 * b + 24, k=str(b))))
+        for lo, hi, kk in ((0, 64, k2[0]), (64, 96, k2[1])):
+            for i1 in range(4):
+                mm(a("N%d" % b, slice(lo, hi), slice(8, 32), i1), a("nr", al, slice(c + 4 * lo + i1, c + 4 * hi, 4), k=kk), a("CN", k="012"))
 
-    def part0(b):
-        N, k = "N%d" % b, str(b)
-        t1, dO, dP = a("t1", R, b, k=k), (T.dd[0:96, b, 0:8, :], ["dd" + k]), (T.dd[0:96, b, 8:16, :], ["dd" + k])
-        tt(t1, a(N, R, slice(16, 24), al), ot(b), A.mult)
-        tt(dO, a(N, R, slice(8, 16), al), ot(b), A.subtract)
-        tt(dP, a(N, R, slice(24, 32), al), t1, A.add)
-
-    def part1(b, nv=2):
+    def find_ops(b, nv):
         C, N, k = "C%d" % b, "N%d" % b, str(b)
-        ts(a(C, R, slice(32, 48), al), a(C, R, slice(0, 16), al), 8.5, A.is_ge)
-        tt(a("hd", R, b, k=k), a(C, R, slice(32, 48), al), a("dd", R, b, k=k), A.mult)
-        tt((T.PO[0:96, b], ["PO" + k]), a(N, R, slice(0, 16), al), a("hd", R, b, k=k), A.add)
-        pads("TP", b, pt(b), nv)
-        tolist("L%d" % b, 0, "TP", b)
+        t1, hh, hd = a("t1", R, b, k=k), a(C, R, slice(32, 48), al), a("hd", R, b, k=k)
+        dO, dP, dd = (T.dd[0:96, b, 0:8, :], ["ddO" + k]), (T.dd[0:96, b, 8:16, :], ["ddP" + k]), (T.dd[0:96, b], ["ddO" + k, "ddP" + k])
+        po = (T.PO[0:96, b], ["PO" + k])
+        return {"st": lambda: start(b), "C": lambda: tform(C, 0, 16, "ge", b, a("G8", k="01")),
+                "t1": lambda: tt(t1, a(N, R, slice(16, 24), al), ot(b), A.mult),
+                "dO": lambda: tt(dO, a(N, R, slice(8, 16), al), ot(b), A.subtract),
+                "dP": lambda: tt(dP, a(N, R, slice(24, 32), al), t1, A.add),
+                "hh": lambda: ts(hh, a(C, R, slice(0, 16), al), 8.5, A.is_ge),
+                "hd": lambda: tt(hd, hh, dd, A.mult),
+                "PO": lambda: tt(po, a(N, R, slice(0, 16), al), hd, A.add),
+                "pd": lambda: pads("TP", b, pt(b), nv),
+                "ls": lambda: tolist("L%d" % b, 0, "TP", b),
+                "LP": lambda: cp(l24("LP", b), cols("L%d" % b, 0, 24))}
 
-    def part2(b):
-        cp(l24("LP", b), cols("L%d" % b, 0, 24))
+    def wants(b):
+        k = str(b)
+        PO, PI = (lambda j: (T.PO[0:96, b, j], ["PO" + k])), (lambda j: (T.PI[0:96, b, j], ["PI" + k]))
+        f = lambda nm: a(nm, R, b, k=k)
+        return [lambda: cp((T.PI[0:96, b], ["PI" + k]), (T.PO[0:96, b], ["PO" + k])),
+                lambda: tt(f("fl"), PO(1), PI(1), A.subtract),
+                lambda: tt(f("df"), PI(0), PI(1), A.subtract),
+                lambda: tt(f("d2"), f("df"), f("df"), A.mult),
+                lambda: ts(f("ne"), f("d2"), 9437184.0, A.not_equal, 4.0, A.mult),
+                lambda: tt(a("wt", R, slice(32 * b, 32 * b + 32), k=k), f("fl"), f("ne"), A.mult)]
 
     def late_constants():
         for j, i, k in ((3, 8, 9), (4, 7, 1), (5, 10, 11), (6, 1, 11)):
@@ -303,8 +324,8 @@ def rank_program(g, core, T, topo):
         act(co(9), pi(10), scale=6240.0)
         act(co(13), co(8), bias=co(9))
         act(a("CK"), g8, scale=co(3))
-        act(cols("CP", 0, 8), g8, scale=co(4))
-        act(cols("CP", 8, 16), g8, scale=co(5))
+        act(cols("CP", 0, 8, k="0"), g8, scale=co(4))
+        act(cols("CP", 8, 16, k="1"), g8, scale=co(5))
         ts(a("BL"), a("kg"), gi, A.is_equal)
         act(a("CB1"), a("BL"), scale=co(4))
         act(a("CB2"), a("BL"), scale=co(5))
@@ -317,59 +338,69 @@ def rank_program(g, core, T, topo):
         ts(a("dumL"), a("dm0"), pm, A.add)
 
     for t in range(3):
-        prev = None
         for q in range(4):
             for b in range(2):
-                start(b)
-                if prev is not None:
-                    part1(prev)
-                tform("C%d" % b, 0, 16, "ge", b, a("G8"))
-                part0(b)
-                if prev is not None:
-                    part2(prev)
-                prev = b
+                cur_, prv_ = find_ops(b, NV), find_ops(1 - b, NV)
+                for x in SEQ:
+                    if x[-1] != "'":
+                        cur_[x]()
+                    elif q + b > 0:
+                        prv_[x[:-1]]()
             if t == 0 and q == 0:
                 late_constants()
+        fin = find_ops(1, NV)
+        for x in SEQ:
+            if x in ("hh'", "hd'", "PO'"):
+                fin[x[:-1]]()
         pads("TO", 0, ot(0), 0)
         tolist("L0", 64, "TO", 0)
-        part1(1, 4)
+        w0, w1 = wants(0), wants(1)
+        w0[0]()
+        w1[0]()
+        w0[1]()
+        pads("TP", 1, pt(1), 4, w1[1:3])
+        tolist("L1", 0, "TP", 1)
         act(half("RA", 0), ind(info(0, PL), l24("LP", 0)))
         pads("TO", 1, ot(1), 0)
         tolist("L0", 88, "TO", 1)
-        part2(1)
+        w0[2]()
+        w1[3]()
+        w0[3]()
+        cp(l24("LO", 0), cols("L0", 64, 88))
+        w0[4]()
+        w1[4]()
+        cp(cols("CC", 0, 96), a("DUMC"))
+        w1[5]()
+        w0[5]()
+        fin["LP"]()
         act(half("RA", 1), ind(info(0, PL), l24("LP", 1)))
-
-        x01 = ["PO0", "PO1"]
-        cp((T.PI[0:96], ["PI"]), (T.PO[0:96], x01))
-        tt(a("fl", R), (T.PO[0:96, :, 1], x01), (T.PI[0:96, :, 1], ["PI"]), A.subtract)
-        tt(a("df", R), (T.PI[0:96, :, 0], ["PI"]), (T.PI[0:96, :, 1], ["PI"]), A.subtract)
-        tt(a("d2", R), a("df", R), a("df", R), A.mult)
-        ts(a("ne", R), a("d2", R), 9437184.0, A.not_equal, 4.0, A.mult)
-        tt(a("wt", R), a("fl", R), a("ne", R), A.mult)
-        run("v", lambda: g.vector.tensor_tensor_scan(T.cs[0:96, :], T.mk[0:96, :], T.wt[0:96, :], 0.0, A.mult, A.add), [a("cs")], [a("mk"), a("wt")])
-        cp(a("LO", k="01"), cols("L0", 64, 112))
+        run("v", lambda: g.vector.tensor_tensor_scan(T.cs[0:96, :], T.mk[0:96, :], T.wt[0:96, :], 0.0, A.mult, A.add), [a("cs")], [a("mk"), a("wt", k="01")])
+        cp(l24("LO", 1), cols("L0", 88, 112))
         for b in range(2):
-            act(half("RB", b), ind((T.Z[:], ["Z", "Za", "Zb", "Zc", "Zd"]), l24("LO", b)))
+            act(half("RB", b), ind(zz, l24("LO", b)))
         mm(a("XA", R, slice(0, 64)), a("I96", R), a("cs", R), True, False)
         for i1 in range(4):
             mm(a("XA", R, slice(i1, 64, 4)), a("S96", R), a("cs", R, slice(3, 64, 4)), False, False)
             mm(a("XA", R, slice(32 + i1, 64, 4)), a("O96", R), a("cs", R, slice(3, 32, 4)), False, i1 == 3)
-        tt(a("rk", R), a("XA", R, slice(0, 64)), a("nb1", R), A.subtract)
-        tt(a("wd", R), a("wt", R), a("rk", R), A.mult)
-        tt(a("de", R), a("wd", R), a("nbj", R), A.add)
+        h32 = lambda nm, b, k: (T[nm][0:96, 32 * b:32 * b + 32], [nm + k])
         for b in range(2):
-            pads("TP", b, (T.de[0:96, b], ["de"]), 4)
+            tt(h32("rk", b, str(b)), h32("XA", b, ""), h32("nb1", b, ""), A.subtract)
+        for b in range(2):
+            tt(h32("wd", b, str(b)), h32("wt", b, str(b)), h32("rk", b, str(b)), A.mult)
+        for b in range(2):
+            tt(a("de", R, b, k=str(b)), h32("wd", b, str(b)), h32("nbj", b, ""), A.add)
+        for b in range(2):
+            pads("TP", b, a("de", R, b, k=str(b)), 4)
             tolist("L1", 24 * b, "TP", b)
-        cp(cols("CC", 0, 96), a("DUMC"))
         cp(a("LD"), cols("L1", 0, 48))
-        tt(ind(a("CC"), a("LD"))[:1] + (["CC"],), a("RA", k="01"), (T.RB[:], ["RB0", "RB1", "LD"]), A.add)
+        tt((T.CC[:].indirect(T.LD[:]), ["CC"]), a("RA", k="01"), (T.RB[:], ["RB0", "RB1", "LD"]), A.add)
         for b in range(2):
             tform("XB", 8 * b, 8, "RA", b, a("CK"))
         for b in range(2):
             pads("TK", b, a("XB", R, slice(8 * b, 8 * b + 8), al), 0)
             tolist("L0", 24 * b, "TK", b)
         for i in range(16):
-            mm(a("L1", slice(0, 6), slice(i, 256, 16)), a("CC", al, slice(i, 96, 16)), a("CP"))
+            mm(a("L1", slice(0, 6), slice(i, 256, 16)), a("CC", al, slice(i, 96, 16)), a("CP", k="01"))
         mm(cols("XA", 128, 224), a("CB1"), cols("CC", 0, 96))
         mm(cols("XA", 224, 320), a("CB2"), cols("CC", 0, 96))
         act(a("L6", slice(0, 6)), a("L1", slice(0, 6), slice(0, 256)))
@@ -383,51 +414,52 @@ def rank_program(g, core, T, topo):
         def addw(b):
             ts(half("DD", b), half("DD", b), 8.0, A.min, -8.0, A.max)
             dma("g", half("WW", b), half("DD", b), accum_op=A.add)
+        if t < 2:
+            sendx(t + 1)
         pull(0)
         addw(0)
         cp(a("RU"), cols("XA", 128, 320))
         pull(1)
         cp(a("Lf"), cols("L1", 256, 268))
-        SN = 9
-        for k in range(12):
-            ts(a("eq", al, k, k=AZ[k]), a("RU"), col("Lf", k), A.is_equal)
-            if k < SN:
-                act(a("jk"), a("eq", al, k, k=AZ[k]), acc=cols("cnt", k, k + 1, k=AZ[k]))
+        for k in range(6):
+            for w in range(2):
+                ts(cols("eq", 384 * k + 192 * w, 384 * k + 192 * w + 192, k=AZ[2 * k + w]), a("RU"), (T.Lf[:, 6 * w + k:6 * w + k + 1], ["Lf"]), A.is_equal)
+            if k < 4:
+                act(cols("jk", 384 * k, 384 * k + 384, k=AZ[k]), cols("eq", 384 * k, 384 * k + 384, k=AZ[2 * k:2 * k + 2]), acc=col("tot", k))
         addw(1)
-        for k in range(SN, 12):
-            run("v", lambda k=k: g.vector.tensor_reduce(T.cnt[:, k:k + 1], T.eq[:, k, :], AxisListType.X, A.add), [a("cnt", k=AZ[k])], [a("eq", k=AZ[k])])
-        c0, c1 = cols("cnt", 0, 6, k=AZ[:6]), cols("cnt", 6, 12, k=AZ[6:12])
-        tt(cols("tot", 0, 6), c0, c1, A.add)
-        tt(cols("tot", 6, 12), c0, c1, A.add)
-        ts(a("nk"), a("tot"), 2.5, A.is_ge)
-        tt(a("tk"), a("nk"), a("dumL"), A.mult)
-        tt(a("Lq"), a("Lf"), a("tk"), A.max)
+        for k in range(4, 6):
+            run("v", lambda k=k: g.vector.tensor_reduce(T.tot[:, k:k + 1], T.eq[:, 384 * k:384 * k + 384], AxisListType.X, A.add),
+                [col("tot", k)], [cols("eq", 0, 1, k=AZ[2 * k:2 * k + 2])])
+        ts(a("nk"), cols("tot", 0, 6, k=AZ[:6]), 2.5, A.is_ge)
+        for w in range(2):
+            tt(cols("tk", 6 * w, 6 * w + 6, k=str(w)), a("nk"), cols("dumL", 6 * w, 6 * w + 6), A.mult)
+        tt(a("Lq"), a("Lf"), a("tk", k="01"), A.max)
         cp(cols("LE", 0, 12, k="0"), a("Lq"))
         cp(cols("LE", 12, 18, k="1"), cols("Lq", 0, 6))
         le0, le1 = cols("LE", 0, 12, k="0"), cols("LE", 6, 18, k="01")
 
         def put(win, src):
-            run("v", lambda: g.vector.tensor_copy(T[win][:].indirect(le1[0]), src[0]), [a(win)], [src, le1])
+            run("v", lambda: g.vector.tensor_copy(win[0].indirect(le1[0]), src[0]), [win], [src, le1])
         if t < 2:
-            act(a("gn"), ind(a("NX"), le0))
-            cp(a("gx"), ind(a("XN"), le0))
-            put("NX", a("gn"))
-            put("XN", a("gx"))
+            act(a("gn"), ind(NX, le0))
+            cp(a("gx"), ind(XN, le0))
+            put(NX, a("gn"))
+            put(XN, a("gx"))
             if t == 1:
-                n8 = lambda nm, r, lo, hi: a(nm, slice(r, 128, 16), slice(lo, hi))
+                n8 = lambda nm, r, lo, hi: (T[nm][r:128:16, lo:hi], NX[1] if nm == "NX" else [nm])
                 dma("g", n8("N32", 0, 0, W), n8("NX", 0, 0, W))
                 dma("g", n8("N32", 0, W, PL), n8("NX", 7, W, PL))
                 dma("g", n8("N32", 0, 0, PL), n8("NX", 1, 0, PL), accum_op=A.add, max_dma_last_dim=4096)
         else:
             cp(a("g32"), ind(a("N32"), le0))
-            put("N32", a("g32"))
+            put(a("N32"), a("g32"))
             dma("y", ext(T.yn[:]), a("N32", slice(0, 128, 16), slice(0, PL)))
             dma("s", ext(T.yw[:]), a("WW", k="01"))
             cp(lo_, a("LP", k="01"))
             cp(hi_, a("LO", k="01"))
-            tt(cols("yco", 0, 48), lo_, hi_, A.min)
-            tt(cols("yco", 48, 96), lo_, hi_, A.max)
-            ts(cols("yco", 48, 96), cols("yco", 48, 96), -3072.0, A.add)
-            dma("s", ext(T.yc[:]), a("yco"))
+            tt(cols("yco", 0, 48, k="0"), lo_, hi_, A.min)
+            tt(a("cd"), lo_, hi_, A.max)
+            ts(cols("yco", 48, 96, k="1"), a("cd"), -3072.0, A.add)
+            dma("s", ext(T.yc[:]), a("yco", k="01"))
     for sem, val in total.items():
         need("g", sem, val)

from concourse.mybir import AluOpType as A, ActivationFunctionType as F, AxisListType

W, K, PL, DUM = 3072, 768, 6144, 6336
F4, B2, I4, U2 = "float32", "bfloat16", "int32", "uint16"
SCRATCH = {}
for names, shape, dtype in (
        ("XS XF0 XF1 XF2", [W], B2), ("XN NX", [DUM], B2), ("INFO Z", [PL], B2), ("N32", [DUM], F4), ("WW DD", [K], F4),
        ("nb_", [24, 16], I4), ("nbf", [24, 16], F4), ("ld2 lt2", [24, 2, 16], F4), ("fr", [384], F4), ("LX", [384], U2),
        ("memc froc", [192], I4), ("curc", [96], I4), ("typc", [48], I4), ("cl yco", [96], F4), ("cd cx cp cq", [48], F4), ("ti", [4, 192], I4),
        ("T0 T1 TL M0 M1 M01 MT1 MT0 ML1 ML0 NM0 NM1 FH FL", [192], B2), ("ZR", [384], B2),
        ("pc", [8], I4), ("pf", [8], F4), ("kr kg BL", [128], F4), ("tb", [192], F4), ("mk nbj nb1", [64], F4), ("dm0 dumL", [12], F4),
        ("pi co", [16], F4), ("hm", [2], F4), ("CN", [24], B2), ("CK", [8], B2), ("CP G8", [16], B2), ("CB1 CB2", [128], B2), ("Mk", [4], F4),
        ("DL", [24], F4), ("S96 I96 O96 DUMC", [96], B2), ("I6", [6], F4),
        ("PO", [2, 2, 8, 4], F4), ("PI", [2, 2, 8, 4], I4), ("LP LO LD LK", [48], U2), ("ge nr RA RB", [K], B2),
        ("t1", [2, 8, 4], F4), ("dd hd", [2, 16, 4], F4), ("TP TO TK", [2, 8, 4, 4], F4),
        ("fl df d2 ne de", [2, 8, 4], F4), ("wt cs", [64], B2), ("rk wd", [64], F4), ("CC", [1536], B2),
        ("RU", [192], U2), ("L6", [256], F4), ("Lf tk Lq", [12], F4), ("tot nk", [6], F4), ("eq", [2304], B2), ("jk", [1536], B2),
        ("gx gn", [192], B2), ("g32", [192], F4), ("LE", [18], U2)):
    for nm in names.split():
        SCRATCH[nm] = ("sbuf", [128] + shape, dtype)
PSUMS = ("N0", "N1", "C0", "C1", "XB", "L0", "L1", "XA")
for nm in PSUMS:
    SCRATCH[nm] = ("psum", [128, 512] if nm in ("L0", "L1", "XA") else [128, 128, 4], F4)
SEMAPHORES = ["qv", "qp", "qs", "qg", "xl", "xa0", "xa1", "xa2"] + ["e%d" % k for k in range(12)] + ["d%d" % k for k in range(60)]
AZ = "abcdefghijklmnopqrstuvwxyz"
SEQ, NV = "st C PO' pd' ls' t1 dO dP hh LP' hd".split(), 2


def rank_program(g, core, T, topo):
    rank = T.rank_of(core)
    if rank is None:
        return
    eng = {"v": g.vector, "p": g.tensor, "s": g.scalar, "g": g, "y": g.sync}
    total, snap, last, reads, nd = {}, {}, {}, {}, {"d": 0, "e": 0}
    know = {q: {} for q in eng}

    def a(name, *idx, k=""):
        t = T[name]
        return (t[idx] if idx else t[:], [name + c for c in k] if k else [name])

    def ind(win, off):
        return (win[0].indirect(off[0]), win[1] + off[1])

    def need(q, sem, val):
        kn = know[q]
        if kn.get(sem, 0) >= val:
            return
        eng[q].wait_ge(T.sem[sem], val)
        for s2, v2 in snap.get((sem, val), {}).items():
            kn[s2] = max(kn.get(s2, 0), v2)
        kn[sem] = max(kn.get(sem, 0), val)

    def deps(q, rd, wr, acc=False):
        for key in rd + wr:
            w = last.get(key)
            if w is not None and not (acc and w[2] == q and key in wr):
                need(q, w[0], w[1])
            if key in PSUMS or key in wr:
                for s2, (v2, q2) in list(reads.get(key, {}).items()):
                    if q2 != q or s2[0] in "de":
                        need(q, s2, v2)

    def done(q, sem, val, rd, wr):
        m = dict(know[q])
        m[sem] = val
        snap[(sem, val)] = m
        for key in wr:
            last[key] = (sem, val, q)
            reads[key] = {}
        for key in rd:
            if key not in wr:
                reads.setdefault(key, {})[sem] = (val, q)

    def run(q, fn, outs, ins, acc=False):
        rd = [x for i in ins for x in i[1]]
        wr = [x for o in outs for x in o[1]]
        deps(q, rd, wr, acc)
        sem = "q" + q
        total[sem] = total.get(sem, 0) + 1
        fn().then_inc(T.sem[sem], 1)
        done(q, sem, total[sem], rd, wr)

    def dma(q, out, in_, **kw):
        deps(q, in_[1], out[1])
        c = "e" if q == "g" else "d"
        sem = "%s%d" % (c, nd[c])
        nd[c] += 1
        total[sem] = 16
        eng[q].dma_start(out[0], in_[0], **kw).then_inc(T.sem[sem], 16)
        done(q, sem, 16, in_[1], out[1])

    def tt(out, i0, i1, op):
        run("v", lambda: g.vector.tensor_tensor(out[0], i0[0], i1[0], op), [out], [i0, i1])

    def ts(out, i0, s1, op0, s2=None, op1=None):
        ins = [i0] + [s for s in (s1, s2) if isinstance(s, tuple)]
        x1 = s1[0] if isinstance(s1, tuple) else s1
        x2 = s2[0] if isinstance(s2, tuple) else s2
        more = [x2, op0] if op1 is None else [x2, op0, op1]
        run("v", lambda: g.vector.tensor_scalar(out[0], i0[0], x1, *more), [out], ins)

    def cp(out, i0):
        run("v", lambda: g.vector.tensor_copy(out[0], i0[0]), [out], [i0])

    def fill(out, v):
        run("v", lambda: g.vector.memset(out[0], v), [out], [])

    def act(out, i0, scale=None, bias=None, acc=None):
        kw, ins, outs = {}, [i0], [out]
        for nm, x in (("scale", scale), ("bias", bias)):
            if isinstance(x, tuple):
                ins.append(x)
                kw[nm] = x[0]
            elif x is not None:
                kw[nm] = x
        if acc is not None:
            outs.append(acc)
            kw["accum_out"] = acc[0]
        fn = F.Identity if isinstance(bias, tuple) else F.Copy
        run("s", lambda: g.scalar.activation(out[0], i0[0], fn, **kw), outs, ins)

    def mm(out, lhsT, rhs, start=True, stop=True):
        run("p", lambda: g.tensor.matmul(out[0], lhsT[0], rhs[0], start, stop), [out], [lhsT, rhs], acc=True)

    def iota(out, pattern, base, cm, **kw):
        run("g", lambda: g.iota(out[0], pattern, base, cm, **kw), [out], [])

    ext = lambda ap: (ap, [])
    al, R = slice(None), slice(0, 96)
    cols = lambda nm, lo, hi, k="": a(nm, al, slice(lo, hi), k=k)
    col = lambda nm, j: a(nm, al, slice(j, j + 1), k=AZ[j])
    half = lambda nm, b: cols(nm, 384 * b, 384 * b + 384, k=str(b))
    l24 = lambda nm, b: cols(nm, 24 * b, 24 * b + 24, k=str(b))

    dma("s", a("nb_"), ext(T.nxt[:]))
    dma("y", a("memc"), ext(T.mem[:]))
    dma("s", a("curc"), ext(T.cur[:]))
    dma("y", a("froc"), ext(T.fro[:]))
    dma("s", a("typc"), ext(T.typ[:]))
    dma("y", a("XS"), ext(T.x[:]))

    fl_ = {"allow_small_or_imprecise_dtypes": True}
    iota(col("pc", 0), [[0, 1]], 0, 1)
    iota(a("tb"), [[64, 3], [0, 64]], 0, 0, **fl_)
    iota(a("TL"), [[0, 3], [1, 64]], 0, 0, **fl_)
    iota(a("kr"), [[1, 128]], 0, 0, **fl_)
    dma("g", a("WW", k="01"), ext(T.w0[:]))
    iota(a("kg"), [[1, 8], [0, 16]], 0, 0, **fl_)
    iota(a("mk"), [[0, 16], [1, 4]], 0, 0, **fl_)
    iota(a("nbj"), [[384, 2], [0, 8], [1, 4]], 768, 4, **fl_)
    iota(a("nb1"), [[384, 2], [0, 8], [1, 4]], 769, 4, **fl_)
    iota(a("dm0"), [[96, 2], [16, 6]], 6144, 0, **fl_)
    for j, op in ((1, (15, A.bitwise_and)),
                  (2, (4, A.arith_shift_right)),
                  (3, (3, A.bitwise_and)), (4, (2, A.arith_shift_right)),
                  (5, (4, A.arith_shift_right, 1, A.bitwise_and))):
        ts(col("pc", j), col("pc", 0), *op)
    cp(cols("pf", 0, 6, k=AZ[:6]), cols("pc", 0, 6, k=AZ[:6]))
    p0, pm, gi = col("pf", 0), col("pf", 1), col("pf", 2)
    ts(col("pf", 6), pm, 192.0, A.mult)
    ts(col("hm", 0), col("pf", 5), -1.0, A.mult, 1.0, A.add)
    ts(a("T0"), a("tb"), col("pf", 6), A.add)
    ts(a("T1"), a("T0"), 3072.0, A.add)
    act(cols("L0", 0, 192), a("T0"))
    act(cols("L0", 192, 384), a("T1"))
    act(cols("L1", 0, 192), a("TL"))
    fill(a("ZR"), 0.0)
    ts(a("pi", k=AZ[:16]), cols("kr", 0, 16), pm, A.is_equal)
    ts(cols("G8", 0, 8, k="0"), cols("kr", 0, 8), gi, A.is_equal)
    co, pi = (lambda j: col("co", j)), (lambda j: col("pi", j))
    g8 = cols("G8", 0, 8, k="0")
    act(co(7), pi(4), scale=0.25)
    act(co(1), pi(0), bias=pi(1))
    act(co(0), co(1), bias=co(7))
    act(co(10), pi(2), bias=pi(3))
    act(co(11), co(10), bias=pi(5))
    act(co(12), co(0), scale=-1.0)
    act(co(2), co(11), bias=co(12))
    act(cols("CN", 0, 8, k="0"), g8, scale=co(0))
    act(cols("CN", 8, 16, k="1"), g8, scale=pi(6))
    act(cols("CN", 16, 24, k="2"), g8, scale=co(2))
    act(cols("G8", 8, 16, k="1"), g8)
    ts(a("Mk"), cols("kr", 0, 4), col("pf", 3), A.is_equal)
    ts(a("DL"), cols("kr", 0, 24), col("pf", 4), A.is_equal)

    ti = lambda j: a("ti", al, j, al, k=str(j))
    ts(ti(0), a("memc"), 1, A.bitwise_and)
    ts(ti(1), a("memc"), 1, A.arith_shift_right)
    cp(a("M0"), ti(0))
    cp(a("M1"), ti(1))
    cp(a("nbf"), a("nb_"))
    tt(a("MT1"), a("M1"), cols("L0", 192, 384), A.mult)
    tt(a("MT0"), a("M0"), cols("L0", 0, 192), A.mult)
    tt(a("ML1"), a("M1"), cols("L1", 0, 192), A.mult)
    tt(a("ML0"), a("M0"), cols("L1", 0, 192), A.mult)
    act(a("ld2", al, al, 0, al, k="0"), a("nbf"), scale=col("hm", 0))
    act(a("ld2", al, al, 1, al, k="1"), a("nbf"), scale=col("pf", 5))
    act(a("NM0"), a("M0"), scale=-1.0, bias=1.0)
    act(a("NM1"), a("M1"), scale=-1.0, bias=1.0)
    act(cols("L1", 192, 384), a("M1"), scale=0.25)
    lo_, hi_ = cols("cl", 0, 48, k="0"), cols("cl", 48, 96, k="1")
    cp(lo_, cols("curc", 0, 48))
    ts(hi_, cols("curc", 48, 96), 3072.0, A.add)
    ts(ti(2), a("froc"), 6, A.arith_shift_right)
    tt(a("cd"), hi_, lo_, A.subtract)
    ts(ti(3), a("froc"), 63, A.bitwise_and)
    tt(a("cx"), a("cd"), a("typc"), A.mult)
    ts(a("FH"), ti(2), 64.0, A.mult)
    tt(a("cp"), lo_, a("cx"), A.add)
    tt(a("cq"), hi_, a("cx"), A.subtract)
    cp(a("FL"), ti(3))
    cp(a("LP", k="01"), a("cp"))
    cp(a("LO", k="01"), a("cq"))
    tt(a("M01"), a("M0"), cols("L1", 192, 384), A.mult)
    for n in range(6):
        dma("y", (T.INFO[10 + n:128:16, :], ["INFO" + AZ[20 + n]]), a("ZR"))
    for r, lo, hi in ((0, "T0", "T1"), (1, "TL", "TL"), (7, "T1", "T0"), (4, "M1", "M0"), (2, "MT1", "MT0"), (3, "ML1", "ML0"), (6, "NM1", "NM0"),
                      (8, "FH", "FH"), (9, "FL", "FL"), (5, "M01", "M01")):
        for h, nm in enumerate((lo, hi)):
            dma("sy"[h], (T.INFO[r:128:16, W * h:W * h + W], ["INFO" + AZ[2 * r + h]]), a(nm))
    info = lambda lo, hi: cols("INFO", lo, hi, k=AZ)

    run("v", lambda: g.vector.transpose(T.lt2[:], T.ld2[:]), [a("lt2")], [a("ld2", k="01")])
    lx = lambda h: cols("LX", 192 * h, 192 * h + 192, k=str(h))
    for h in range(2):
        for ch in range(8 * h, 8 * h + 8):
            tt(cols("fr", 24 * ch, 24 * ch + 24, k=AZ[ch]), a("lt2", al, al, 0, ch), a("lt2", al, al, 1, ch), A.add)
        cp(lx(h), cols("fr", 192 * h, 192 * h + 192, k=AZ[8 * h:8 * h + 8]))
    fill(cols("NX", PL, DUM, k="2"), 0.0)
    fill(cols("XN", PL, DUM, k="2"), 0.0)
    for h in range(2):
        cp(cols("XN", W * h, W * h + W, k=str(h)), ind(a("XS"), lx(h)))
        act(cols("NX", W * h, W * h + W, k=str(h)), ind(info(W * h, W * h + W), lx(h)))
        if h == 0:
            cp(half("RB", 0), ind(info(0, PL), l24("LO", 0)))
            act(half("RB", 1), ind(info(0, PL), l24("LO", 1)))
    XN, NX = a("XN", k="012"), a("NX", k="012")

    def sendx(t):
        deps("g", ["XS"], [])
        if t:
            need("g", "xl", total["xl"])
        dst = T.cores[(rank - 1 - t) % 8]
        rid, pid = topo.addr(dst, core)
        n = len(topo.engines(core, dst))
        sem = "xa%d" % t
        total["xl"] = total.get("xl", 0) + n
        total[sem] = n
        g.remote_dma(T["XF%d" % t][:], T.XS[:], T.sem[sem], T.sem.xl, pid, rid, topo.mask(core, dst))
        last["XF%d" % t] = (sem, n, "-")
    sendx(0)
    iota(a("Z"), [[0, PL]], 0, 0, **fl_)
    iota(a("N32"), [[0, DUM]], 0, 0, **fl_)
    for k, (r, h, nm) in enumerate(((10, 0, "T0"), (10, 1, "T1"), (11, 0, "TL"), (11, 1, "TL"))):
        deps("y", [], ["Z"])
        dma("y", (T.Z[r:128:16, W * h:W * h + W], ["Z" + AZ[k]]), a(nm))
    zz = (T.Z[:], ["Z", "Za", "Zb", "Zc", "Zd"])

    def tform(bank, c0, n, rowbuf, b, rhs):
        for i1 in range(4):
            mm(a(bank, R, slice(c0, c0 + n), i1), a(rowbuf, al, slice(384 * b + i1, 384 * b + 384, 4), k=str(b)), rhs)

    def pads(tp, b, src, nv, between=()):
        for i0 in range(4):
            if i0 in (1, 3) and between:
                between[i0 // 2]()
            out, m = a(tp, R, b, al, i0, al, k=str(4 * b + i0)), a("Mk", R, slice(i0, i0 + 1))
            if i0 < nv:
                ts(out, src, m, A.mult)
            else:
                act(out, src, scale=m)

    def tolist(bank, c0, tp, b):
        mm(cols(bank, c0, c0 + 24), (T[tp][0:96, b], [tp + str(4 * b + i) for i in range(4)]), a("DL", R))

    ot = lambda b: (T.PO[0:96, b, 0], ["PO%d" % b])
    pt = lambda b: (T.PO[0:96, b, 1], ["PO%d" % b])
    for b in range(2):
        tform("XB", 8 * b, 8, "RB", b, cols("CN", 0, 8, k="0"))
        cp(ot(b), a("XB", R, slice(8 * b, 8 * b + 8), al))

    def start(b):
        off, gew, ww = l24("LP", b), half("ge", b), half("WW", b)
        tt(gew, ind(XN, off), ww, A.is_ge)
        act(a("N%d" % b, R, slice(0, 8), al), ot(b))
        c, k2 = 384 * b, (str(b), "xy"[b])
        act(cols("nr", c, c + 256, k=k2[0]), ind(NX, cols("LP", 24 * b, 24 * b + 16, k=str(b))))
        act(cols("nr", c + 256, c + 384, k=k2[1]), ind(NX, cols("LP", 24 * b + 16, 24 * b + 24, k=str(b))))
        for lo, hi, kk in ((0, 64, k2[0]), (64, 96, k2[1])):
            for i1 in range(4):
                mm(a("N%d" % b, slice(lo, hi), slice(8, 32), i1), a("nr", al, slice(c + 4 * lo + i1, c + 4 * hi, 4), k=kk), a("CN", k="012"))

    def find_ops(b, nv):
        C, N, k = "C%d" % b, "N%d" % b, str(b)
        t1, hh, hd = a("t1", R, b, k=k), a(C, R, slice(32, 48), al), a("hd", R, b, k=k)
        dO, dP, dd = (T.dd[0:96, b, 0:8, :], ["ddO" + k]), (T.dd[0:96, b, 8:16, :], ["ddP" + k]), (T.dd[0:96, b], ["ddO" + k, "ddP" + k])
        po = (T.PO[0:96, b], ["PO" + k])
        return {"st": lambda: start(b), "C": lambda: tform(C, 0, 16, "ge", b, a("G8", k="01")),
                "t1": lambda: tt(t1, a(N, R, slice(16, 24), al), ot(b), A.mult),
                "dO": lambda: tt(dO, a(N, R, slice(8, 16), al), ot(b), A.subtract),
                "dP": lambda: tt(dP, a(N, R, slice(24, 32), al), t1, A.add),
                "hh": lambda: ts(hh, a(C, R, slice(0, 16), al), 8.5, A.is_ge),
                "hd": lambda: tt(hd, hh, dd, A.mult),
                "PO": lambda: tt(po, a(N, R, slice(0, 16), al), hd, A.add),
                "pd": lambda: pads("TP", b, pt(b), nv),
                "ls": lambda: tolist("L%d" % b, 0, "TP", b),
                "LP": lambda: cp(l24("LP", b), cols("L%d" % b, 0, 24))}

    def wants(b):
        k = str(b)
        PO, PI = (lambda j: (T.PO[0:96, b, j], ["PO" + k])), (lambda j: (T.PI[0:96, b, j], ["PI" + k]))
        f = lambda nm: a(nm, R, b, k=k)
        return [lambda: cp((T.PI[0:96, b], ["PI" + k]), (T.PO[0:96, b], ["PO" + k])),
                lambda: tt(f("fl"), PO(1), PI(1), A.subtract),
                lambda: tt(f("df"), PI(0), PI(1), A.subtract),
                lambda: tt(f("d2"), f("df"), f("df"), A.mult),
                lambda: ts(f("ne"), f("d2"), 9437184.0, A.not_equal, 4.0, A.mult),
                lambda: tt(a("wt", R, slice(32 * b, 32 * b + 32), k=k), f("fl"), f("ne"), A.mult)]

    def late_constants():
        for j, i, k in ((3, 8, 9), (4, 7, 1), (5, 10, 11), (6, 1, 11)):
            act(co(j), pi(i), bias=pi(k))
        act(co(8), pi(7), scale=6144.0)
        act(co(9), pi(10), scale=6240.0)
        act(co(13), co(8), bias=co(9))
        act(a("CK"), g8, scale=co(3))
        act(cols("CP", 0, 8, k="0"), g8, scale=co(4))
        act(cols("CP", 8, 16, k="1"), g8, scale=co(5))
        ts(a("BL"), a("kg"), gi, A.is_equal)
        act(a("CB1"), a("BL"), scale=co(4))
        act(a("CB2"), a("BL"), scale=co(5))
        ts(a("mk"), a("mk"), 0.5, A.is_ge)
        ts(a("I96"), cols("kr", 0, 96), p0, A.is_equal)
        ts(a("S96"), cols("kr", 0, 96), p0, A.is_gt)
        fill(a("O96"), 1.0)
        ts(a("I6"), cols("kr", 0, 6), p0, A.is_equal)
        ts(a("DUMC"), cols("kr", 0, 96), co(6), A.mult, co(13), A.add)
        ts(a("dumL"), a("dm0"), pm, A.add)

    for t in range(3):
        for q in range(4):
            for b in range(2):
                cur_, prv_ = find_ops(b, NV), find_ops(1 - b, NV)
                for x in SEQ:
                    if x[-1] != "'":
                        cur_[x]()
                    elif q + b > 0:
                        prv_[x[:-1]]()
            if t == 0 and q == 0:
                late_constants()
        fin = find_ops(1, NV)
        for x in SEQ:
            if x in ("hh'", "hd'", "PO'"):
                fin[x[:-1]]()
        pads("TO", 0, ot(0), 0)
        tolist("L0", 64, "TO", 0)
        w0, w1 = wants(0), wants(1)
        w0[0]()
        w1[0]()
        w0[1]()
        pads("TP", 1, pt(1), 4, w1[1:3])
        tolist("L1", 0, "TP", 1)
        act(half("RA", 0), ind(info(0, PL), l24("LP", 0)))
        pads("TO", 1, ot(1), 0)
        tolist("L0", 88, "TO", 1)
        w0[2]()
        w1[3]()
        w0[3]()
        cp(l24("LO", 0), cols("L0", 64, 88))
        w0[4]()
        w1[4]()
        cp(cols("CC", 0, 96), a("DUMC"))
        w1[5]()
        w0[5]()
        fin["LP"]()
        act(half("RA", 1), ind(info(0, PL), l24("LP", 1)))
        run("v", lambda: g.vector.tensor_tensor_scan(T.cs[0:96, :], T.mk[0:96, :], T.wt[0:96, :], 0.0, A.mult, A.add), [a("cs")], [a("mk"), a("wt", k="01")])
        cp(l24("LO", 1), cols("L0", 88, 112))
        for b in range(2):
            act(half("RB", b), ind(zz, l24("LO", b)))
        mm(a("XA", R, slice(0, 64)), a("I96", R), a("cs", R), True, False)
        for i1 in range(4):
            mm(a("XA", R, slice(i1, 64, 4)), a("S96", R), a("cs", R, slice(3, 64, 4)), False, False)
            mm(a("XA", R, slice(32 + i1, 64, 4)), a("O96", R), a("cs", R, slice(3, 32, 4)), False, i1 == 3)
        h32 = lambda nm, b, k: (T[nm][0:96, 32 * b:32 * b + 32], [nm + k])
        for b in range(2):
            tt(h32("rk", b, str(b)), h32("XA", b, ""), h32("nb1", b, ""), A.subtract)
        for b in range(2):
            tt(h32("wd", b, str(b)), h32("wt", b, str(b)), h32("rk", b, str(b)), A.mult)
        for b in range(2):
            tt(a("de", R, b, k=str(b)), h32("wd", b, str(b)), h32("nbj", b, ""), A.add)
        for b in range(2):
            pads("TP", b, a("de", R, b, k=str(b)), 4)
            tolist("L1", 24 * b, "TP", b)
        cp(a("LD"), cols("L1", 0, 48))
        tt((T.CC[:].indirect(T.LD[:]), ["CC"]), a("RA", k="01"), (T.RB[:], ["RB0", "RB1", "LD"]), A.add)
        for b in range(2):
            tform("XB", 8 * b, 8, "RA", b, a("CK"))
        for b in range(2):
            pads("TK", b, a("XB", R, slice(8 * b, 8 * b + 8), al), 0)
            tolist("L0", 24 * b, "TK", b)
        for i in range(16):
            mm(a("L1", slice(0, 6), slice(i, 256, 16)), a("CC", al, slice(i, 96, 16)), a("CP", k="01"))
        mm(cols("XA", 128, 224), a("CB1"), cols("CC", 0, 96))
        mm(cols("XA", 224, 320), a("CB2"), cols("CC", 0, 96))
        act(a("L6", slice(0, 6)), a("L1", slice(0, 6), slice(0, 256)))
        for k in range(2):
            mm(cols("L1", 256 + 6 * k, 262 + 6 * k), a("L6", slice(0, 6), slice(128 * k, 128 * k + 128)), a("I6", slice(0, 6)))
        cp(a("LK"), cols("L0", 0, 48))

        def pull(b):
            tt(half("DD", b), ind(a("XF%d" % t), cols("LK", 24 * b, 24 * b + 24)), half("WW", b), A.subtract)

        def addw(b):
            ts(half("DD", b), half("DD", b), 8.0, A.min, -8.0, A.max)
            dma("g", half("WW", b), half("DD", b), accum_op=A.add)
        if t < 2:
            sendx(t + 1)
        pull(0)
        addw(0)
        cp(a("RU"), cols("XA", 128, 320))
        pull(1)
        cp(a("Lf"), cols("L1", 256, 268))
        for k in range(6):
            for w in range(2):
                ts(cols("eq", 384 * k + 192 * w, 384 * k + 192 * w + 192, k=AZ[2 * k + w]), a("RU"), (T.Lf[:, 6 * w + k:6 * w + k + 1], ["Lf"]), A.is_equal)
            if k < 4:
                act(cols("jk", 384 * k, 384 * k + 384, k=AZ[k]), cols("eq", 384 * k, 384 * k + 384, k=AZ[2 * k:2 * k + 2]), acc=col("tot", k))
        addw(1)
        for k in range(4, 6):
            run("v", lambda k=k: g.vector.tensor_reduce(T.tot[:, k:k + 1], T.eq[:, 384 * k:384 * k + 384], AxisListType.X, A.add),
                [col("tot", k)], [cols("eq", 0, 1, k=AZ[2 * k:2 * k + 2])])
        ts(a("nk"), cols("tot", 0, 6, k=AZ[:6]), 2.5, A.is_ge)
        for w in range(2):
            tt(cols("tk", 6 * w, 6 * w + 6, k=str(w)), a("nk"), cols("dumL", 6 * w, 6 * w + 6), A.mult)
        tt(a("Lq"), a("Lf"), a("tk", k="01"), A.max)
        cp(cols("LE", 0, 12, k="0"), a("Lq"))
        cp(cols("LE", 12, 18, k="1"), cols("Lq", 0, 6))
        le0, le1 = cols("LE", 0, 12, k="0"), cols("LE", 6, 18, k="01")

        def put(win, src):
            run("v", lambda: g.vector.tensor_copy(win[0].indirect(le1[0]), src[0]), [win], [src, le1])
        if t < 2:
            act(a("gn"), ind(NX, le0))
            cp(a("gx"), ind(XN, le0))
            put(NX, a("gn"))
            put(XN, a("gx"))
            if t == 1:
                n8 = lambda nm, r, lo, hi: (T[nm][r:128:16, lo:hi], NX[1] if nm == "NX" else [nm])
                dma("g", n8("N32", 0, 0, W), n8("NX", 0, 0, W))
                dma("g", n8("N32", 0, W, PL), n8("NX", 7, W, PL))
                dma("g", n8("N32", 0, 0, PL), n8("NX", 1, 0, PL), accum_op=A.add, max_dma_last_dim=4096)
        else:
            cp(a("g32"), ind(a("N32"), le0))
            put(a("N32"), a("g32"))
            dma("y", ext(T.yn[:]), a("N32", slice(0, 128, 16), slice(0, PL)))
            dma("s", ext(T.yw[:]), a("WW", k="01"))
            cp(lo_, a("LP", k="01"))
            cp(hi_, a("LO", k="01"))
            tt(cols("yco", 0, 48, k="0"), lo_, hi_, A.min)
            tt(a("cd"), lo_, hi_, A.max)
            ts(cols("yco", 48, 96, k="1"), a("cd"), -3072.0, A.add)
            dma("s", ext(T.yc[:]), a("yco", k="01"))
    for sem, val in total.items():
        need("g", sem, val)
